import numpy as np
import ml_dtypes


def mxq(x, axis, fmt="e4m3"):
    dtype, down = {"e4m3": (ml_dtypes.float8_e4m3fn, 7), "e5m2": (ml_dtypes.float8_e5m2, 14)}[fmt]
    v = np.moveaxis(np.asarray(x, np.float32).astype(ml_dtypes.bfloat16).astype(np.float64), axis, -1)
    blocks = v.reshape(v.shape[:-1] + (-1, 32))
    amax = np.abs(blocks).max(-1, keepdims=True)
    byte = np.maximum(np.where(amax > 0, np.frexp(amax)[1] - 1 + 127, 0) - down, 1)
    scale = np.exp2(byte - 127.0)
    codes = (blocks / scale).astype(np.float32).astype(dtype).astype(np.float64)
    return np.moveaxis((codes * scale).reshape(v.shape), -1, axis)


WIDE = False


def mx_kscale(k):
    if not WIDE:
        return np.ones(k)
    levels = np.array([10, -10, 5, -5, 0])
    if k % 512:
        return np.exp2(np.random.permutation(np.resize(levels, k // 32))).repeat(32)
    a = np.empty((k // 512, 16))
    for p in range(k // 512):
        a[p, :8] = np.random.permutation(np.resize(levels, 8))
        for g in range(8):
            far = levels[np.abs(levels - a[p, g]) >= 10]
            a[p, g + 8] = far[np.random.randint(len(far))]
    return np.exp2(a.ravel()).repeat(32)


BF16 = ml_dtypes.bfloat16


def bf(x):
    return np.asarray(x, np.float32).astype(BF16)


def f64(x):
    return np.asarray(x).astype(np.float64)

E4M3FN = np.array([(-1.0 if i & 128 else 1.0) * ((1.0 + (i & 7) / 8.0) * 2.0 ** (((i >> 3) & 15) - 7) if i & 120 else (i & 7) * 2.0 ** -9) for i in range(256)])


def e4m3fn_bytes(y):
    return np.clip(np.asarray(y, np.float64), -448.0, 448.0).astype(np.float32).astype(ml_dtypes.float8_e4m3fn).view(np.uint8)


def e4m3fn_values(b):
    return E4M3FN[b]

def planes(Y):
    n, m = Y.shape
    b = f64(bf(Y)).reshape(n // 32, 32, m)
    amax = np.abs(b).max(1)
    byte = np.clip(np.where(amax > 0, np.frexp(amax)[1] - 1 + 127 - 7, 1), 1, 254)
    codes = (b * np.exp2(127.0 - byte)[:, None, :]).reshape(n, m).astype(np.float32).astype(ml_dtypes.float8_e4m3fn).view(np.uint8)
    words = codes.reshape(n // 512, 128, 4, m).transpose(0, 1, 3, 2)
    return np.ascontiguousarray(words), np.ascontiguousarray(byte.astype(np.uint8).reshape(n // 512, 16, m))


T, K, N = 1024, 2048, 1024

F8_MAX = 448.0
MEAN_SPREAD = 0.5

def setup_inputs():
    s = mx_kscale(K)
    size = np.exp(0.4 * np.random.randn(1, K))
    raw = size * (np.random.randn(T, K) + MEAN_SPREAD * np.random.randn(1, K)) * s
    F_mean = bf(raw.mean(axis=0, keepdims=True))
    dev = raw - f64(F_mean)
    F_scale = (np.abs(dev).max(axis=0, keepdims=True) / F8_MAX).astype(np.float32)
    F_bytes = e4m3fn_bytes(dev / f64(F_scale))
    W = bf(np.random.randn(K, N) / np.sqrt(K) / s[:, None])
    b = bf(0.4 * np.random.randn(1, N))
    spread = np.exp(0.7 * np.random.randn(1, N))
    x0 = bf(spread * np.random.randn(T, N))
    x = bf(0.8 * spread * np.random.randn(T, N))
    return {"F_bytes": F_bytes, "F_scale": F_scale, "F_mean": F_mean,
            "W": W, "b": b, "x0": x0, "x": x}

def reference(F_bytes, F_scale, F_mean, W, b, x0, x):
    F = e4m3fn_values(F_bytes) * f64(F_scale) + f64(F_mean)
    z = mxq(F, 1, "e4m3") @ mxq(f64(W), 0, "e4m3")
    y = f64(x0) * (z + f64(b)) + f64(x)
    words, scales = planes(y.T)
    return y, words, scales

@@ -1,0 +1,381 @@
+from contextlib import ExitStack
+
+import concourse.mybir as mybir
+from concourse.masks import make_identity
+
+T, K, N = 1024, 2048, 1024
+FLOPS = 2 * T * K * N
+
+F32 = mybir.dt.float32
+BF16 = mybir.dt.bfloat16
+U32 = mybir.dt.uint32
+I32 = mybir.dt.int32
+U8 = mybir.dt.uint8
+FP8 = mybir.dt.float8_e4m3fn
+FP8X4 = mybir.dt.float8_e4m3fn_x4
+ALU = mybir.AluOpType
+ACT = mybir.ActivationFunctionType
+
+P = 128
+PACK = 4
+SPAN = 512
+PASSES = K // SPAN
+TILES = SPAN // P
+
+
+def tile_centred_store_feature_cross_b15_kernel(tc, F_bytes, F_scale, F_mean, W, b, x0, x, out_0, out_1, out_2):
+    nc = tc.nc
+    with ExitStack() as ctx:
+        keep = ctx.enter_context(tc.tile_pool(name="keep", bufs=1))
+        work = ctx.enter_context(tc.tile_pool(name="work", bufs=2))
+        psum = ctx.enter_context(tc.psum_pool(name="psum", bufs=1))
+        ctx.enter_context(tc.manual_schedule())
+
+        free_banks = list(range(8))
+        held = {}
+
+        def take_bank(key, shape, dtype):
+            held[key] = free_banks.pop(0)
+            bank = psum.tile(shape, dtype, name="bank", tag="bank%d" % held[key])
+            return bank
+
+        def give_bank(key):
+            free_banks.append(held[key])
+
+        ident32 = keep.tile([P, P], F32, name="ident32")
+        ident16 = keep.tile([P, P], BF16, name="ident16")
+        b_rows = keep.tile([P, P], BF16, name="b_rows")
+        make_identity(nc, ident32[:])
+        nc.gpsimd.memset(b_rows[:], 0.0)
+
+        scale = keep.tile([P, PASSES, PACK], F32, name="scale")
+        mean = keep.tile([P, PASSES, PACK], BF16, name="mean")
+        b_cols = keep.tile([P, N // P], F32, name="b_cols")
+        w_raw, f_raw, x0_sb, x_sb = {}, {}, {}, {}
+
+        def load_w(G, g):
+            w_raw[G, g] = keep.tile([P, PACK, SPAN], BF16, name="w_raw", bufs=2 * PASSES)
+            src = W[g * SPAN : (g + 1) * SPAN, G * SPAN : (G + 1) * SPAN]
+            nc.sync.dma_start(out=w_raw[G, g][:], in_=src.rearrange("(p t) n -> p t n", t=PACK))
+
+        def load_f(h, g):
+            f_raw[h, g] = keep.tile([P, TILES, SPAN], U8, name="f_raw", bufs=2 * PASSES)
+            src = F_bytes[h * SPAN : (h + 1) * SPAN, g * SPAN : (g + 1) * SPAN]
+            nc.sync.dma_start(out=f_raw[h, g][:], in_=src.rearrange("(i p) k -> p i k", p=P))
+
+        def load_rows(store, src, name, h):
+            store[h] = keep.tile([P, TILES, N], BF16, name=name, bufs=2)
+            nc.sync.dma_start(out=store[h][:], in_=src[h * SPAN : (h + 1) * SPAN, :].rearrange("(i p) n -> p i n", p=P))
+
+        load_w(0, 0)
+        load_f(0, 0)
+        nc.sync.dma_start(out=mean[:], in_=F_mean.rearrange("o (g p t) -> p (o g) t", p=P, t=PACK))
+        nc.sync.dma_start(out=scale[:], in_=F_scale.rearrange("o (g p t) -> p (o g) t", p=P, t=PACK))
+        for g in range(1, PASSES):
+            load_w(0, g)
+            load_f(0, g)
+        nc.sync.dma_start(out=b_rows[0 : N // P, :], in_=b.rearrange("o (j p) -> (o j) p", p=P))
+        load_rows(x0_sb, x0, "x0_sb", 0)
+        load_w(1, 0)
+        load_f(1, 0)
+        load_f(1, 1)
+        load_w(1, 1)
+        load_rows(x_sb, x, "x_sb", 0)
+        for g in range(2, PASSES):
+            load_f(1, g)
+            load_w(1, g)
+        load_rows(x0_sb, x0, "x0_sb", 1)
+        load_rows(x_sb, x, "x_sb", 1)
+
+        nc.scalar.activation(out=ident16[:], in_=ident32[:], func=ACT.Identity)
+
+        wide, f_banks, planes, grouped = {}, {}, {}, {}
+        codes, scales = {}, {}
+        x0_bank, yt_bank = {}, {}
+        x0_t, acc, v_t, y_bank, y_sb, y16, y_grouped = {}, {}, {}, {}, {}, {}, {}
+        y_scales = keep.tile([P, N // SPAN, T], U8, name="y_scales", align_bytes=64)
+
+        def widen(h, g):
+            wide[h, g] = work.tile([P, TILES, SPAN], BF16, name="wide", bufs=3)
+            nc.scalar.copy(out=wide[h, g][:], in_=f_raw[h, g][:].bitcast(FP8))
+
+        def turn_f(h, g):
+            for u in range(2):
+                f_banks[h, g, u] = take_bank(("f", h, g, u), [P, TILES, P], F32)
+                for i in range(TILES):
+                    words = wide[h, g][:, i, :].bitcast(F32)
+                    nc.tensor.transpose(f_banks[h, g, u][:, i, :], words[:, u : 2 * P : 2], ident32[:])
+
+        def affine(h, g):
+            planes["f", h, g] = work.tile([P, PACK, SPAN], BF16, name="f_planes", bufs=4)
+            for u in range(2):
+                pairs = f_banks[h, g, u][:].rearrange("p i m -> p (i m)").bitcast(BF16).rearrange("p (c e) -> p e c", e=2)
+                for e in range(2):
+                    t = 2 * u + e
+                    nc.scalar.activation(
+                        out=planes["f", h, g][:, t, :], in_=pairs[:, e, :], func=ACT.Identity,
+                        scale=scale[:, g, t : t + 1], bias=mean[:, g, t : t + 1],
+                    )
+                give_bank(("f", h, g, u))
+
+        def interleave(key, on_scalar=False):
+            src = w_raw[key[1:]] if key[0] == "w" else planes[key]
+            grouped[key] = work.tile([P, SPAN, PACK], BF16, name="grouped", bufs=3, align_bytes=64)
+            copy = nc.scalar.copy if on_scalar else nc.vector.tensor_copy
+            copy(
+                out=grouped[key][:].rearrange("p (c i) t -> p c t i", i=4),
+                in_=src[:].rearrange("p t (c i) -> p c t i", i=4),
+            )
+
+        def quantise(key):
+            codes[key] = keep.tile([P, SPAN], U32, name="codes", bufs=4 * PASSES, align_bytes=64)
+            scales[key] = keep.tile([P, SPAN], U8, name="scales", bufs=4 * PASSES, align_bytes=64)
+            nc.vector.quantize_mx(out=codes[key][:].bitcast(FP8X4), scales=scales[key][:], in_=grouped[key][:].rearrange("p c t -> p (c t)"))
+
+        def bias_columns():
+            bank = take_bank("b", [P, P], BF16)
+            nc.tensor.transpose(bank[:], b_rows[:], ident16[:])
+            nc.scalar.copy(out=b_cols[:], in_=bank[:, 0 : N // P])
+            give_bank("b")
+
+        def turn_x0(G, h, pair):
+            bank = take_bank(("x0", G, h, pair), [P, 2, SPAN], BF16)
+            x0_bank[G, h, pair] = bank
+            for jj in range(2):
+                col = G * SPAN + (2 * pair + jj) * P
+                for i in range(TILES):
+                    nc.tensor.transpose(bank[:, jj, i * P : (i + 1) * P], x0_sb[h][:, i, col : col + P], ident16[:])
+
+        def empty_x0(G, h, pair):
+            x0_t[G, h, pair] = work.tile([P, 2, SPAN], BF16, name="x0_t", bufs=4)
+            nc.scalar.copy(out=x0_t[G, h, pair][:], in_=x0_bank[G, h, pair][:])
+            give_bank(("x0", G, h, pair))
+
+        def multiply(G, h, j, g):
+            if g == 0:
+                acc[G, h, j] = take_bank(("acc", G, h, j), [P, SPAN], F32)
+            cols = slice(j * P, (j + 1) * P)
+            nc.tensor.matmul_mx(
+                out=acc[G, h, j][:],
+                lhsT=codes["w", G, g][:, cols].bitcast(FP8X4), lhsT_scale=scales["w", G, g][:, cols],
+                rhs=codes["f", h, g][:].bitcast(FP8X4), rhs_scale=scales["f", h, g][:],
+                start=(g == 0), stop=(g == PASSES - 1),
+            )
+
+        def multiply_pass(G, h, g):
+            for j in range(TILES):
+                multiply(G, h, j, g)
+
+        def multiply_tile(G, h, j):
+            for g in range(PASSES):
+                multiply(G, h, j, g)
+
+        def cross(G, h, j):
+            v_t[G, h, j] = work.tile([P, SPAN], F32, name="v_t", bufs=8)
+            col = G * TILES + j
+            nc.vector.scalar_tensor_tensor(
+                out=v_t[G, h, j][:], in0=acc[G, h, j][:], scalar=b_cols[:, col : col + 1],
+                in1=x0_t[G, h, j // 2][:, j % 2, :], op0=ALU.add, op1=ALU.mult,
+            )
+            give_bank(("acc", G, h, j))
+
+        def turn_back(G, h, i):
+            y_bank[G, h, i] = take_bank(("y", G, h, i), [P, SPAN], F32)
+            for j in range(TILES):
+                nc.tensor.transpose(y_bank[G, h, i][:, j * P : (j + 1) * P], v_t[G, h, j][:, i * P : (i + 1) * P], ident32[:])
+
+        def add_x(G, h, i):
+            y_sb[G, h, i] = work.tile([P, SPAN], F32, name="y_sb", bufs=5)
+            nc.vector.tensor_tensor(out=y_sb[G, h, i][:], in0=y_bank[G, h, i][:], in1=x_sb[h][:, i, G * SPAN : (G + 1) * SPAN], op=ALU.add)
+            give_bank(("y", G, h, i))
+            row = h * SPAN + i * P
+            nc.sync.dma_start(out=out_0[row : row + P, G * SPAN : (G + 1) * SPAN], in_=y_sb[G, h, i][:])
+
+        def round_y(G, h, i, on_vector=False):
+            y16[G, h, i] = work.tile([P, 2, P, 2], BF16, name="y16", bufs=6)
+            copy = nc.vector.tensor_copy if on_vector else nc.scalar.copy
+            copy(out=y16[G, h, i][:], in_=y_sb[G, h, i][:].rearrange("p (m u e) -> p u m e", u=2, e=2))
+
+        def turn_y(G, h, first, count):
+            bank = take_bank(("yt", G, h, first), [P, count, 2, P], F32)
+            yt_bank[G, h, first] = bank
+            for ii in range(count):
+                for u in range(2):
+                    words = y16[G, h, first + ii][:, u, :, :].rearrange("p m e -> p (m e)").bitcast(F32)
+                    nc.tensor.transpose(bank[:, ii, u, :], words, ident32[:])
+
+        def empty_y(G, h, first, count):
+            if first == 0:
+                y_grouped[G, h] = work.tile([P, SPAN, PACK], BF16, name="y_grouped", bufs=4, align_bytes=64)
+            dst = y_grouped[G, h][:, first * P : (first + count) * P, :].rearrange("p c t -> p (c t)").bitcast(F32)
+            nc.scalar.copy(out=dst.rearrange("p (i m u) -> p i m u", i=count, u=2), in_=yt_bank[G, h, first][:].rearrange("p i u m -> p i m u"))
+            give_bank(("yt", G, h, first))
+
+        def quantise_y(G, h, first, count):
+            y_codes = work.tile([P, count * P], U32, name="y_codes", bufs=5, align_bytes=64)
+            rows = slice(h * SPAN + first * P, h * SPAN + (first + count) * P)
+            nc.vector.quantize_mx(
+                out=y_codes[:].bitcast(FP8X4), scales=y_scales[:, G, rows],
+                in_=y_grouped[G, h][:, first * P : (first + count) * P, :].rearrange("p c t -> p (c t)"),
+            )
+            dst = out_1[G, :, rows, :].rearrange("p m t -> p (m t)")
+            nc.sync.dma_start(out=dst.bitcast(I32), in_=y_codes[:].bitcast(I32))
+
+        SF = False
+        def x0_pair(G, h, pair):
+            turn_x0(G, h, pair)
+            empty_x0(G, h, pair)
+
+        def y_pair(G, h, first):
+            turn_y(G, h, first, 2)
+            empty_y(G, h, first, 2)
+
+        widen(0, 0)
+        turn_f(0, 0)
+        widen(0, 1)
+        turn_f(0, 1)
+        interleave(("w", 0, 0))
+        for g in range(1, PASSES):
+            interleave(("w", 0, g))
+            quantise(("w", 0, g - 1))
+        affine(0, 0)
+        widen(0, 2)
+        turn_f(0, 2)
+        affine(0, 1)
+        widen(0, 3)
+        turn_f(0, 3)
+        interleave(("f", 0, 0))
+        quantise(("w", 0, 3))
+        affine(0, 2)
+        interleave(("f", 0, 1))
+        quantise(("f", 0, 0))
+        multiply_pass(0, 0, 0)
+        affine(0, 3)
+        bias_columns()
+        interleave(("w", 1, 0))
+        quantise(("f", 0, 1))
+        turn_x0(0, 0, 0)
+        multiply_pass(0, 0, 1)
+        widen(1, 0)
+        empty_x0(0, 0, 0)
+        interleave(("f", 0, 2))
+        quantise(("w", 1, 0))
+        x0_pair(0, 0, 1)
+        interleave(("f", 0, 3))
+        quantise(("f", 0, 2))
+        multiply_pass(0, 0, 2)
+        turn_f(1, 0)
+        widen(1, 1)
+        interleave(("w", 1, 1))
+        quantise(("f", 0, 3))
+        multiply_pass(0, 0, 3)
+        interleave(("w", 1, 2))
+        quantise(("w", 1, 1))
+        affine(1, 0)
+        turn_f(1, 1)
+        widen(1, 2)
+        for j in range(TILES):
+            cross(0, 0, j)
+        quantise(("w", 1, 2))
+        multiply_pass(1, 0, 0)
+        affine(1, 1)
+        interleave(("w", 1, 3))
+        turn_back(0, 0, 0)
+        turn_back(0, 0, 1)
+        add_x(0, 0, 0)
+        add_x(0, 0, 1)
+        multiply_pass(1, 0, 1)
+        turn_f(1, 2)
+        widen(1, 3)
+        quantise(("w", 1, 3))
+        interleave(("f", 1, 0))
+        multiply_pass(1, 0, 2)
+        turn_back(0, 0, 2)
+        turn_back(0, 0, 3)
+        add_x(0, 0, 2)
+        add_x(0, 0, 3)
+        affine(1, 2)
+        multiply_pass(1, 0, 3)
+        x0_pair(1, 0, 0)
+        x0_pair(1, 0, 1)
+        quantise(("f", 1, 0))
+        interleave(("f", 1, 1))
+        turn_f(1, 3)
+        for j in range(TILES):
+            cross(1, 0, j)
+        affine(1, 3)
+        for i in range(TILES):
+            round_y(0, 0, i)
+        quantise(("f", 1, 1))
+        multiply_pass(0, 1, 0)
+        interleave(("f", 1, 2))
+        turn_back(1, 0, 0)
+        turn_back(1, 0, 1)
+        add_x(1, 0, 0)
+        add_x(1, 0, 1)
+        multiply_pass(0, 1, 1)
+        x0_pair(0, 1, 0)
+        x0_pair(0, 1, 1)
+        quantise(("f", 1, 2))
+        interleave(("f", 1, 3), SF)
+        for j in range(2):
+            for g in range(2):
+                multiply(1, 1, j, g)
+        turn_back(1, 0, 2)
+        turn_back(1, 0, 3)
+        add_x(1, 0, 2)
+        add_x(1, 0, 3)
+        multiply_pass(0, 1, 2)
+        y_pair(0, 0, 0)
+        y_pair(0, 0, 2)
+        multiply(1, 1, 0, 2)
+        multiply(1, 1, 1, 2)
+        quantise(("f", 1, 3))
+        x0_pair(1, 1, 0)
+        x0_pair(1, 1, 1)
+        for i in range(TILES):
+            round_y(1, 0, i)
+        multiply_pass(0, 1, 3)
+        multiply(1, 1, 0, 3)
+        multiply(1, 1, 1, 3)
+        quantise_y(0, 0, 0, 4)
+        for j in range(TILES):
+            cross(0, 1, j)
+        multiply_tile(1, 1, 2)
+        y_pair(1, 0, 0)
+        y_pair(1, 0, 2)
+        for j in range(3):
+            cross(1, 1, j)
+        turn_back(0, 1, 0)
+        turn_back(0, 1, 1)
+        multiply_tile(1, 1, 3)
+        turn_back(0, 1, 2)
+        turn_back(0, 1, 3)
+        add_x(0, 1, 0)
+        add_x(0, 1, 1)
+        cross(1, 1, 3)
+        add_x(0, 1, 2)
+        add_x(0, 1, 3)
+        for i in range(TILES):
+            round_y(0, 1, i)
+            turn_back(1, 1, i)
+            add_x(1, 1, i)
+        turn_y(0, 1, 0, 2)
+        turn_y(0, 1, 2, 2)
+        round_y(1, 1, 0)
+        round_y(1, 1, 1)
+        round_y(1, 1, 2, True)
+        round_y(1, 1, 3, True)
+        quantise_y(1, 0, 0, 4)
+        turn_y(1, 1, 0, 2)
+        turn_y(1, 1, 2, 2)
+        empty_y(0, 1, 0, 2)
+        empty_y(0, 1, 2, 2)
+        quantise_y(0, 1, 0, 4)
+        empty_y(1, 1, 0, 2)
+        empty_y(1, 1, 2, 2)
+        quantise_y(1, 1, 0, 2)
+        quantise_y(1, 1, 2, 2)
+        for q in range(4):
+            dst = out_2[:, 4 * q : 4 * q + 4, :].rearrange("g r m -> r g m")
+            nc.sync.dma_start(out=dst.bitcast(I32), in_=y_scales[32 * q : 32 * q + 4, :, :].bitcast(I32))

@@ -17,6 +17,8 @@ ALU = mybir.AluOpType
 ACT = mybir.ActivationFunctionType
 
 P = 128
+YB = 6
+PB = 4
 PACK = 4
 SPAN = 512
 PASSES = K // SPAN
@@ -31,26 +33,17 @@ def tile_centred_store_feature_cross_b15_kernel(tc, F_bytes, F_scale, F_mean, W,
         psum = ctx.enter_context(tc.psum_pool(name="psum", bufs=1))
         ctx.enter_context(tc.manual_schedule())
 
-        free_banks = list(range(8))
-        held = {}
-
-        def take_bank(key, shape, dtype):
-            held[key] = free_banks.pop(0)
-            bank = psum.tile(shape, dtype, name="bank", tag="bank%d" % held[key])
+        def take_bank(number, shape, dtype):
+            bank = psum.tile(shape, dtype, name="bank", tag="bank%d" % number)
             return bank
 
-        def give_bank(key):
-            free_banks.append(held[key])
-
         ident32 = keep.tile([P, P], F32, name="ident32")
-        ident16 = keep.tile([P, P], BF16, name="ident16")
-        b_rows = keep.tile([P, P], BF16, name="b_rows")
         make_identity(nc, ident32[:])
-        nc.gpsimd.memset(b_rows[:], 0.0)
 
         scale = keep.tile([P, PASSES, PACK], F32, name="scale")
         mean = keep.tile([P, PASSES, PACK], BF16, name="mean")
-        b_cols = keep.tile([P, N // P], F32, name="b_cols")
+        b16 = keep.tile([P, N // (2 * P), 2], BF16, name="b16")
+        b_cols = keep.tile([P, N // (2 * P), 2], F32, name="b_cols")
         w_raw, f_raw, x0_sb, x_sb = {}, {}, {}, {}
 
         def load_w(G, g):
@@ -67,47 +60,45 @@ def tile_centred_store_feature_cross_b15_kernel(tc, F_bytes, F_scale, F_mean, W,
             store[h] = keep.tile([P, TILES, N], BF16, name=name, bufs=2)
             nc.sync.dma_start(out=store[h][:], in_=src[h * SPAN : (h + 1) * SPAN, :].rearrange("(i p) n -> p i n", p=P))
 
+        nc.sync.dma_start(out=b16[:], in_=b.rearrange("o (q p e) -> p (o q) e", p=P, e=2))
         load_w(0, 0)
         load_f(0, 0)
+        load_f(0, 1)
+        load_w(0, 1)
         nc.sync.dma_start(out=mean[:], in_=F_mean.rearrange("o (g p t) -> p (o g) t", p=P, t=PACK))
         nc.sync.dma_start(out=scale[:], in_=F_scale.rearrange("o (g p t) -> p (o g) t", p=P, t=PACK))
-        for g in range(1, PASSES):
+        for g in range(2, PASSES):
             load_w(0, g)
             load_f(0, g)
-        nc.sync.dma_start(out=b_rows[0 : N // P, :], in_=b.rearrange("o (j p) -> (o j) p", p=P))
         load_rows(x0_sb, x0, "x0_sb", 0)
-        load_w(1, 0)
-        load_f(1, 0)
-        load_f(1, 1)
-        load_w(1, 1)
-        load_rows(x_sb, x, "x_sb", 0)
-        for g in range(2, PASSES):
-            load_f(1, g)
+        for g in range(PASSES):
             load_w(1, g)
+            load_f(1, g)
         load_rows(x0_sb, x0, "x0_sb", 1)
+        load_rows(x_sb, x, "x_sb", 0)
         load_rows(x_sb, x, "x_sb", 1)
 
-        nc.scalar.activation(out=ident16[:], in_=ident32[:], func=ACT.Identity)
 
         wide, f_banks, planes, grouped = {}, {}, {}, {}
         codes, scales = {}, {}
-        x0_bank, yt_bank = {}, {}
+        x0_bank, yt_bank, done = {}, {}, {}
         x0_t, acc, v_t, y_bank, y_sb, y16, y_grouped = {}, {}, {}, {}, {}, {}, {}
         y_scales = keep.tile([P, N // SPAN, T], U8, name="y_scales", align_bytes=64)
 
-        def widen(h, g):
+        def widen(h, g, on_vector=False):
             wide[h, g] = work.tile([P, TILES, SPAN], BF16, name="wide", bufs=3)
-            nc.scalar.copy(out=wide[h, g][:], in_=f_raw[h, g][:].bitcast(FP8))
+            copy = nc.vector.tensor_copy if on_vector else nc.scalar.copy
+            copy(out=wide[h, g][:], in_=f_raw[h, g][:].bitcast(FP8))
 
-        def turn_f(h, g):
+        def turn_f(h, g, first_bank):
             for u in range(2):
-                f_banks[h, g, u] = take_bank(("f", h, g, u), [P, TILES, P], F32)
+                f_banks[h, g, u] = take_bank(first_bank + u, [P, TILES, P], F32)
                 for i in range(TILES):
                     words = wide[h, g][:, i, :].bitcast(F32)
                     nc.tensor.transpose(f_banks[h, g, u][:, i, :], words[:, u : 2 * P : 2], ident32[:])
 
         def affine(h, g):
-            planes["f", h, g] = work.tile([P, PACK, SPAN], BF16, name="f_planes", bufs=4)
+            planes["f", h, g] = work.tile([P, PACK, SPAN], BF16, name="f_planes", bufs=PB)
             for u in range(2):
                 pairs = f_banks[h, g, u][:].rearrange("p i m -> p (i m)").bitcast(BF16).rearrange("p (c e) -> p e c", e=2)
                 for e in range(2):
@@ -116,100 +107,101 @@ def tile_centred_store_feature_cross_b15_kernel(tc, F_bytes, F_scale, F_mean, W,
                         out=planes["f", h, g][:, t, :], in_=pairs[:, e, :], func=ACT.Identity,
                         scale=scale[:, g, t : t + 1], bias=mean[:, g, t : t + 1],
                     )
-                give_bank(("f", h, g, u))
 
         def interleave(key, on_scalar=False):
-            src = w_raw[key[1:]] if key[0] == "w" else planes[key]
             grouped[key] = work.tile([P, SPAN, PACK], BF16, name="grouped", bufs=3, align_bytes=64)
             copy = nc.scalar.copy if on_scalar else nc.vector.tensor_copy
-            copy(
-                out=grouped[key][:].rearrange("p (c i) t -> p c t i", i=4),
-                in_=src[:].rearrange("p t (c i) -> p c t i", i=4),
-            )
+            if key[0] == "f":
+                copy(
+                    out=grouped[key][:].rearrange("p (c i) t -> p c t i", i=4),
+                    in_=planes[key][:].rearrange("p t (c i) -> p c t i", i=4),
+                )
+            else:
+                for q in range(2):
+                    cols = slice(q * 2 * P, (q + 1) * 2 * P)
+                    copy(
+                        out=grouped[key][:, cols, :].rearrange("p (e c i) t -> p e c t i", e=2, i=4),
+                        in_=w_raw[key[1:]][:, :, cols].rearrange("p t (c i e) -> p e c t i", e=2, i=4),
+                    )
 
         def quantise(key):
             codes[key] = keep.tile([P, SPAN], U32, name="codes", bufs=4 * PASSES, align_bytes=64)
             scales[key] = keep.tile([P, SPAN], U8, name="scales", bufs=4 * PASSES, align_bytes=64)
             nc.vector.quantize_mx(out=codes[key][:].bitcast(FP8X4), scales=scales[key][:], in_=grouped[key][:].rearrange("p c t -> p (c t)"))
 
-        def bias_columns():
-            bank = take_bank("b", [P, P], BF16)
-            nc.tensor.transpose(bank[:], b_rows[:], ident16[:])
-            nc.scalar.copy(out=b_cols[:], in_=bank[:, 0 : N // P])
-            give_bank("b")
+        def turn_x0(G, h, q, first_bank):
+            x0_bank[G, h, q] = take_bank(first_bank + q, [P, TILES, P], F32)
+            col = G * SPAN + q * 2 * P
+            for i in range(TILES):
+                nc.tensor.transpose(x0_bank[G, h, q][:, i, :], x0_sb[h][:, i, col : col + 2 * P].bitcast(F32), ident32[:])
 
-        def turn_x0(G, h, pair):
-            bank = take_bank(("x0", G, h, pair), [P, 2, SPAN], BF16)
-            x0_bank[G, h, pair] = bank
-            for jj in range(2):
-                col = G * SPAN + (2 * pair + jj) * P
-                for i in range(TILES):
-                    nc.tensor.transpose(bank[:, jj, i * P : (i + 1) * P], x0_sb[h][:, i, col : col + P], ident16[:])
+        def empty_x0(G, h, q, on_vector=False):
+            x0_t[G, h, q] = work.tile([P, SPAN, 2], BF16, name="x0_t", bufs=4)
+            copy = nc.vector.tensor_copy if on_vector else nc.scalar.copy
+            copy(out=x0_t[G, h, q][:].rearrange("p c e -> p (c e)").bitcast(F32), in_=x0_bank[G, h, q][:].rearrange("p i m -> p (i m)"))
 
-        def empty_x0(G, h, pair):
-            x0_t[G, h, pair] = work.tile([P, 2, SPAN], BF16, name="x0_t", bufs=4)
-            nc.scalar.copy(out=x0_t[G, h, pair][:], in_=x0_bank[G, h, pair][:])
-            give_bank(("x0", G, h, pair))
-
-        def multiply(G, h, j, g):
-            if g == 0:
-                acc[G, h, j] = take_bank(("acc", G, h, j), [P, SPAN], F32)
+        def multiply(G, h, j, g, bank):
+            done[G, h, j] = done.get((G, h, j), 0) + 1
+            if done[G, h, j] == 1:
+                acc[G, h, j] = take_bank(bank, [P, SPAN], F32)
             cols = slice(j * P, (j + 1) * P)
             nc.tensor.matmul_mx(
                 out=acc[G, h, j][:],
                 lhsT=codes["w", G, g][:, cols].bitcast(FP8X4), lhsT_scale=scales["w", G, g][:, cols],
                 rhs=codes["f", h, g][:].bitcast(FP8X4), rhs_scale=scales["f", h, g][:],
-                start=(g == 0), stop=(g == PASSES - 1),
+                start=(done[G, h, j] == 1), stop=(done[G, h, j] == PASSES),
             )
 
         def multiply_pass(G, h, g):
             for j in range(TILES):
-                multiply(G, h, j, g)
+                multiply(G, h, j, g, j)
 
-        def multiply_tile(G, h, j):
+        def multiply_tile(G, h, j, bank):
             for g in range(PASSES):
-                multiply(G, h, j, g)
+                multiply(G, h, j, g, bank)
 
         def cross(G, h, j):
             v_t[G, h, j] = work.tile([P, SPAN], F32, name="v_t", bufs=8)
-            col = G * TILES + j
             nc.vector.scalar_tensor_tensor(
-                out=v_t[G, h, j][:], in0=acc[G, h, j][:], scalar=b_cols[:, col : col + 1],
-                in1=x0_t[G, h, j // 2][:, j % 2, :], op0=ALU.add, op1=ALU.mult,
+                out=v_t[G, h, j][:], in0=acc[G, h, j][:], scalar=b_cols[:, 2 * G + j // 2, j % 2 : j % 2 + 1],
+                in1=x0_t[G, h, j // 2][:, :, j % 2], op0=ALU.add, op1=ALU.mult,
             )
-            give_bank(("acc", G, h, j))
 
-        def turn_back(G, h, i):
-            y_bank[G, h, i] = take_bank(("y", G, h, i), [P, SPAN], F32)
+        def turn_back(G, h, i, bank):
+            y_bank[G, h, i] = take_bank(bank, [P, SPAN], F32)
             for j in range(TILES):
                 nc.tensor.transpose(y_bank[G, h, i][:, j * P : (j + 1) * P], v_t[G, h, j][:, i * P : (i + 1) * P], ident32[:])
 
         def add_x(G, h, i):
-            y_sb[G, h, i] = work.tile([P, SPAN], F32, name="y_sb", bufs=5)
-            nc.vector.tensor_tensor(out=y_sb[G, h, i][:], in0=y_bank[G, h, i][:], in1=x_sb[h][:, i, G * SPAN : (G + 1) * SPAN], op=ALU.add)
-            give_bank(("y", G, h, i))
+            y_sb[G, h, i] = work.tile([P, SPAN], F32, name="y_sb", bufs=YB)
+            nc.vector.tensor_tensor(
+                out=y_sb[G, h, i][:].rearrange("p (q m e) -> p q m e", q=2, e=2),
+                in0=y_bank[G, h, i][:].rearrange("p (q e m) -> p q m e", q=2, e=2),
+                in1=x_sb[h][:, i, G * SPAN : (G + 1) * SPAN].rearrange("p (q m e) -> p q m e", q=2, e=2),
+                op=ALU.add,
+            )
             row = h * SPAN + i * P
             nc.sync.dma_start(out=out_0[row : row + P, G * SPAN : (G + 1) * SPAN], in_=y_sb[G, h, i][:])
 
         def round_y(G, h, i, on_vector=False):
-            y16[G, h, i] = work.tile([P, 2, P, 2], BF16, name="y16", bufs=6)
+            y16[G, h, i] = work.tile([P, 2, P, 2], BF16, name="y16", bufs=10)
             copy = nc.vector.tensor_copy if on_vector else nc.scalar.copy
             copy(out=y16[G, h, i][:], in_=y_sb[G, h, i][:].rearrange("p (m u e) -> p u m e", u=2, e=2))
 
-        def turn_y(G, h, first, count):
-            bank = take_bank(("yt", G, h, first), [P, count, 2, P], F32)
+        def turn_y(G, h, first, count, number):
+            bank = take_bank(number, [P, count, 2, P], F32)
             yt_bank[G, h, first] = bank
             for ii in range(count):
                 for u in range(2):
                     words = y16[G, h, first + ii][:, u, :, :].rearrange("p m e -> p (m e)").bitcast(F32)
                     nc.tensor.transpose(bank[:, ii, u, :], words, ident32[:])
 
-        def empty_y(G, h, first, count):
+        def empty_y(G, h, first, count, on_vector=False):
             if first == 0:
                 y_grouped[G, h] = work.tile([P, SPAN, PACK], BF16, name="y_grouped", bufs=4, align_bytes=64)
             dst = y_grouped[G, h][:, first * P : (first + count) * P, :].rearrange("p c t -> p (c t)").bitcast(F32)
-            nc.scalar.copy(out=dst.rearrange("p (i m u) -> p i m u", i=count, u=2), in_=yt_bank[G, h, first][:].rearrange("p i u m -> p i m u"))
-            give_bank(("yt", G, h, first))
+            copy = nc.vector.tensor_copy if on_vector else nc.scalar.copy
+            copy(out=dst.rearrange("p (i m u) -> p i m u", i=count, u=2), in_=yt_bank[G, h, first][:].rearrange("p i u m -> p i m u"))
 
         def quantise_y(G, h, first, count):
             y_codes = work.tile([P, count * P], U32, name="y_codes", bufs=5, align_bytes=64)
@@ -221,159 +213,175 @@ def tile_centred_store_feature_cross_b15_kernel(tc, F_bytes, F_scale, F_mean, W,
             dst = out_1[G, :, rows, :].rearrange("p m t -> p (m t)")
             nc.sync.dma_start(out=dst.bitcast(I32), in_=y_codes[:].bitcast(I32))
 
-        SF = False
-        def x0_pair(G, h, pair):
-            turn_x0(G, h, pair)
-            empty_x0(G, h, pair)
+        A, B, C = 0, 4, 6
 
-        def y_pair(G, h, first):
-            turn_y(G, h, first, 2)
-            empty_y(G, h, first, 2)
+        def cross_all(G, h):
+            for j in range(TILES):
+                cross(G, h, j)
 
+        def back2(G, h, first, bank):
+            turn_back(G, h, first, bank)
+            turn_back(G, h, first + 1, bank + 1)
+
+        def add2(G, h, first):
+            add_x(G, h, first)
+            add_x(G, h, first + 1)
+
+        def round2(G, h, first, on_vector=False):
+            round_y(G, h, first, on_vector)
+            round_y(G, h, first + 1, on_vector)
+
+        def turn_x0_both(G, h, bank):
+            turn_x0(G, h, 0, bank)
+            turn_x0(G, h, 1, bank)
+
+        def empty_x0_both(G, h):
+            empty_x0(G, h, 0)
+            empty_x0(G, h, 1)
+
+        def turn_y_both(G, h, bank):
+            turn_y(G, h, 0, 2, bank)
+            turn_y(G, h, 2, 2, bank + 1)
+
+        def empty_y_both(G, h):
+            empty_y(G, h, 0, 2)
+            empty_y(G, h, 2, 2)
+
+        nc.scalar.activation(out=b_cols[:], in_=b16[:], func=ACT.Identity)
         widen(0, 0)
-        turn_f(0, 0)
+        turn_f(0, 0, A)
         widen(0, 1)
-        turn_f(0, 1)
-        interleave(("w", 0, 0))
-        for g in range(1, PASSES):
-            interleave(("w", 0, g))
-            quantise(("w", 0, g - 1))
+        turn_f(0, 1, A + 2)
         affine(0, 0)
         widen(0, 2)
-        turn_f(0, 2)
+        turn_f(0, 2, B)
         affine(0, 1)
         widen(0, 3)
-        turn_f(0, 3)
+        turn_f(0, 3, C)
+        interleave(("w", 0, 0))
+        quantise(("w", 0, 0))
+        interleave(("w", 0, 1))
+        interleave(("w", 0, 2))
+        quantise(("w", 0, 1))
+        interleave(("w", 0, 3))
+        quantise(("w", 0, 2))
         interleave(("f", 0, 0))
         quantise(("w", 0, 3))
         affine(0, 2)
         interleave(("f", 0, 1))
         quantise(("f", 0, 0))
         multiply_pass(0, 0, 0)
+        turn_x0_both(0, 0, B)
         affine(0, 3)
-        bias_columns()
+        widen(1, 0)
         interleave(("w", 1, 0))
         quantise(("f", 0, 1))
-        turn_x0(0, 0, 0)
         multiply_pass(0, 0, 1)
-        widen(1, 0)
-        empty_x0(0, 0, 0)
+        turn_f(1, 0, C)
+        empty_x0_both(0, 0)
+        turn_x0_both(1, 0, B)
+        widen(1, 1)
         interleave(("f", 0, 2))
         quantise(("w", 1, 0))
-        x0_pair(0, 0, 1)
         interleave(("f", 0, 3))
         quantise(("f", 0, 2))
-        multiply_pass(0, 0, 2)
-        turn_f(1, 0)
-        widen(1, 1)
-        interleave(("w", 1, 1))
         quantise(("f", 0, 3))
+        multiply_pass(0, 0, 2)
         multiply_pass(0, 0, 3)
-        interleave(("w", 1, 2))
-        quantise(("w", 1, 1))
         affine(1, 0)
-        turn_f(1, 1)
+        empty_x0_both(1, 0)
+        turn_f(1, 1, B)
+        interleave(("w", 1, 1))
         widen(1, 2)
-        for j in range(TILES):
-            cross(0, 0, j)
-        quantise(("w", 1, 2))
-        multiply_pass(1, 0, 0)
         affine(1, 1)
-        interleave(("w", 1, 3))
-        turn_back(0, 0, 0)
-        turn_back(0, 0, 1)
-        add_x(0, 0, 0)
-        add_x(0, 0, 1)
+        cross_all(0, 0)
+        multiply_pass(1, 0, 0)
+        quantise(("w", 1, 1))
+        back2(0, 0, 0, C)
         multiply_pass(1, 0, 1)
-        turn_f(1, 2)
+        interleave(("w", 1, 2))
+        interleave(("w", 1, 3))
+        quantise(("w", 1, 2))
+        turn_f(1, 2, B)
         widen(1, 3)
-        quantise(("w", 1, 3))
-        interleave(("f", 1, 0))
-        multiply_pass(1, 0, 2)
-        turn_back(0, 0, 2)
-        turn_back(0, 0, 3)
-        add_x(0, 0, 2)
-        add_x(0, 0, 3)
         affine(1, 2)
+        multiply_pass(1, 0, 2)
+        add2(0, 0, 0)
+        quantise(("w", 1, 3))
         multiply_pass(1, 0, 3)
-        x0_pair(1, 0, 0)
-        x0_pair(1, 0, 1)
-        quantise(("f", 1, 0))
-        interleave(("f", 1, 1))
-        turn_f(1, 3)
-        for j in range(TILES):
-            cross(1, 0, j)
+        round2(0, 0, 0)
+        interleave(("f", 1, 0))
+        turn_f(1, 3, B)
+        back2(0, 0, 2, C)
         affine(1, 3)
-        for i in range(TILES):
-            round_y(0, 0, i)
+        cross(1, 0, 0)
+        cross(1, 0, 1)
+        quantise(("f", 1, 0))
+        multiply(0, 1, 0, 0, A)
+        multiply(0, 1, 1, 0, A + 1)
+        interleave(("f", 1, 1))
+        interleave(("f", 1, 3), True)
+        turn_x0_both(0, 1, B)
+        empty_x0_both(0, 1)
+        cross(1, 0, 2)
+        cross(1, 0, 3)
+        multiply(0, 1, 2, 0, A + 2)
+        multiply(0, 1, 3, 0, A + 3)
         quantise(("f", 1, 1))
-        multiply_pass(0, 1, 0)
-        interleave(("f", 1, 2))
-        turn_back(1, 0, 0)
-        turn_back(1, 0, 1)
-        add_x(1, 0, 0)
-        add_x(1, 0, 1)
         multiply_pass(0, 1, 1)
-        x0_pair(0, 1, 0)
-        x0_pair(0, 1, 1)
-        quantise(("f", 1, 2))
-        interleave(("f", 1, 3), SF)
-        for j in range(2):
-            for g in range(2):
-                multiply(1, 1, j, g)
-        turn_back(1, 0, 2)
-        turn_back(1, 0, 3)
-        add_x(1, 0, 2)
-        add_x(1, 0, 3)
-        multiply_pass(0, 1, 2)
-        y_pair(0, 0, 0)
-        y_pair(0, 0, 2)
-        multiply(1, 1, 0, 2)
-        multiply(1, 1, 1, 2)
+        add2(0, 0, 2)
+        interleave(("f", 1, 2))
+        back2(1, 0, 0, C)
         quantise(("f", 1, 3))
-        x0_pair(1, 1, 0)
-        x0_pair(1, 1, 1)
-        for i in range(TILES):
-            round_y(1, 0, i)
+        round2(0, 0, 2)
+        quantise(("f", 1, 2))
+        for g in (0, 1):
+            multiply(1, 1, 0, g, B)
+            multiply(1, 1, 1, g, B + 1)
+        add2(1, 0, 0)
         multiply_pass(0, 1, 3)
-        multiply(1, 1, 0, 3)
-        multiply(1, 1, 1, 3)
+        multiply_pass(0, 1, 2)
+        round2(1, 0, 0)
+        back2(1, 0, 2, C)
+        cross_all(0, 1)
+        turn_x0_both(1, 1, A)
+        empty_x0_both(1, 1)
+        for g in (3, 2):
+            multiply(1, 1, 0, g, B)
+            multiply(1, 1, 1, g, B + 1)
+        add2(1, 0, 2)
+        round2(1, 0, 2)
+        turn_y_both(0, 0, C)
+        empty_y_both(0, 0)
+        multiply_tile(1, 1, 2, A + 2)
+        cross(1, 1, 0)
+        cross(1, 1, 1)
+        back2(0, 1, 0, A)
+        multiply_tile(1, 1, 3, A + 3)
+        turn_y_both(1, 0, B)
+        empty_y_both(1, 0)
+        back2(0, 1, 2, C)
         quantise_y(0, 0, 0, 4)
-        for j in range(TILES):
-            cross(0, 1, j)
-        multiply_tile(1, 1, 2)
-        y_pair(1, 0, 0)
-        y_pair(1, 0, 2)
-        for j in range(3):
-            cross(1, 1, j)
-        turn_back(0, 1, 0)
-        turn_back(0, 1, 1)
-        multiply_tile(1, 1, 3)
-        turn_back(0, 1, 2)
-        turn_back(0, 1, 3)
-        add_x(0, 1, 0)
-        add_x(0, 1, 1)
+        add2(0, 1, 0)
+        round2(0, 1, 0)
+        cross(1, 1, 2)
         cross(1, 1, 3)
-        add_x(0, 1, 2)
-        add_x(0, 1, 3)
-        for i in range(TILES):
-            round_y(0, 1, i)
-            turn_back(1, 1, i)
-            add_x(1, 1, i)
-        turn_y(0, 1, 0, 2)
-        turn_y(0, 1, 2, 2)
-        round_y(1, 1, 0)
-        round_y(1, 1, 1)
-        round_y(1, 1, 2, True)
-        round_y(1, 1, 3, True)
-        quantise_y(1, 0, 0, 4)
-        turn_y(1, 1, 0, 2)
-        turn_y(1, 1, 2, 2)
-        empty_y(0, 1, 0, 2)
-        empty_y(0, 1, 2, 2)
-        quantise_y(0, 1, 0, 4)
+        back2(1, 1, 0, A)
+        back2(1, 1, 2, A + 2)
+        add2(0, 1, 2)
+        round2(0, 1, 2)
+        turn_y_both(0, 1, B)
+        add2(1, 1, 0)
+        round2(1, 1, 0)
+        turn_y(1, 1, 0, 2, C)
+        empty_y_both(0, 1)
+        add2(1, 1, 2)
+        round2(1, 1, 2, True)
+        turn_y(1, 1, 2, 2, C + 1)
         empty_y(1, 1, 0, 2)
-        empty_y(1, 1, 2, 2)
+        quantise_y(1, 0, 0, 4)
+        quantise_y(0, 1, 0, 4)
+        empty_y(1, 1, 2, 2, True)
         quantise_y(1, 1, 0, 2)
         quantise_y(1, 1, 2, 2)
         for q in range(4):

@@ -17,7 +17,7 @@ ALU = mybir.AluOpType
 ACT = mybir.ActivationFunctionType
 
 P = 128
-YB = 6
+YB = 8
 PB = 4
 PACK = 4
 SPAN = 512
@@ -38,12 +38,14 @@ def tile_centred_store_feature_cross_b15_kernel(tc, F_bytes, F_scale, F_mean, W,
             return bank
 
         ident32 = keep.tile([P, P], F32, name="ident32")
+        ident16 = keep.tile([P, P], BF16, name="ident16")
+        b_rows = keep.tile([P, P], BF16, name="b_rows")
         make_identity(nc, ident32[:])
+        nc.gpsimd.memset(b_rows[:], 0.0)
 
         scale = keep.tile([P, PASSES, PACK], F32, name="scale")
         mean = keep.tile([P, PASSES, PACK], BF16, name="mean")
-        b16 = keep.tile([P, N // (2 * P), 2], BF16, name="b16")
-        b_cols = keep.tile([P, N // (2 * P), 2], F32, name="b_cols")
+        b_cols = keep.tile([P, N // P], F32, name="b_cols")
         w_raw, f_raw, x0_sb, x_sb = {}, {}, {}, {}
 
         def load_w(G, g):
@@ -60,13 +62,13 @@ def tile_centred_store_feature_cross_b15_kernel(tc, F_bytes, F_scale, F_mean, W,
             store[h] = keep.tile([P, TILES, N], BF16, name=name, bufs=2)
             nc.sync.dma_start(out=store[h][:], in_=src[h * SPAN : (h + 1) * SPAN, :].rearrange("(i p) n -> p i n", p=P))
 
-        nc.sync.dma_start(out=b16[:], in_=b.rearrange("o (q p e) -> p (o q) e", p=P, e=2))
         load_w(0, 0)
         load_f(0, 0)
         load_f(0, 1)
         load_w(0, 1)
         nc.sync.dma_start(out=mean[:], in_=F_mean.rearrange("o (g p t) -> p (o g) t", p=P, t=PACK))
         nc.sync.dma_start(out=scale[:], in_=F_scale.rearrange("o (g p t) -> p (o g) t", p=P, t=PACK))
+        nc.sync.dma_start(out=b_rows[0 : N // P, :], in_=b.rearrange("o (j p) -> (o j) p", p=P))
         for g in range(2, PASSES):
             load_w(0, g)
             load_f(0, g)
@@ -74,8 +76,10 @@ def tile_centred_store_feature_cross_b15_kernel(tc, F_bytes, F_scale, F_mean, W,
         for g in range(PASSES):
             load_w(1, g)
             load_f(1, g)
-        load_rows(x0_sb, x0, "x0_sb", 1)
         load_rows(x_sb, x, "x_sb", 0)
+        b_spread = keep.tile([P, SPAN], BF16, name="b_spread")
+        nc.sync.dma_start(out=b_spread[:], in_=b[:, SPAN:N].rearrange("o n -> (o n)").partition_broadcast(P))
+        load_rows(x0_sb, x0, "x0_sb", 1)
         load_rows(x_sb, x, "x_sb", 1)
 
 
@@ -109,36 +113,32 @@ def tile_centred_store_feature_cross_b15_kernel(tc, F_bytes, F_scale, F_mean, W,
                     )
 
         def interleave(key, on_scalar=False):
+            src = w_raw[key[1:]] if key[0] == "w" else planes[key]
             grouped[key] = work.tile([P, SPAN, PACK], BF16, name="grouped", bufs=3, align_bytes=64)
-            copy = nc.scalar.copy if on_scalar else nc.vector.tensor_copy
-            if key[0] == "f":
-                copy(
-                    out=grouped[key][:].rearrange("p (c i) t -> p c t i", i=4),
-                    in_=planes[key][:].rearrange("p t (c i) -> p c t i", i=4),
-                )
+            if on_scalar:
+                nc.scalar.copy(out=grouped[key][:], in_=src[:].rearrange("p t c -> p c t"))
             else:
-                for q in range(2):
-                    cols = slice(q * 2 * P, (q + 1) * 2 * P)
-                    copy(
-                        out=grouped[key][:, cols, :].rearrange("p (e c i) t -> p e c t i", e=2, i=4),
-                        in_=w_raw[key[1:]][:, :, cols].rearrange("p t (c i e) -> p e c t i", e=2, i=4),
-                    )
+                nc.vector.tensor_copy(
+                    out=grouped[key][:].rearrange("p (c i) t -> p c t i", i=4),
+                    in_=src[:].rearrange("p t (c i) -> p c t i", i=4),
+                )
 
         def quantise(key):
             codes[key] = keep.tile([P, SPAN], U32, name="codes", bufs=4 * PASSES, align_bytes=64)
             scales[key] = keep.tile([P, SPAN], U8, name="scales", bufs=4 * PASSES, align_bytes=64)
             nc.vector.quantize_mx(out=codes[key][:].bitcast(FP8X4), scales=scales[key][:], in_=grouped[key][:].rearrange("p c t -> p (c t)"))
 
-        def turn_x0(G, h, q, first_bank):
-            x0_bank[G, h, q] = take_bank(first_bank + q, [P, TILES, P], F32)
-            col = G * SPAN + q * 2 * P
-            for i in range(TILES):
-                nc.tensor.transpose(x0_bank[G, h, q][:, i, :], x0_sb[h][:, i, col : col + 2 * P].bitcast(F32), ident32[:])
 
-        def empty_x0(G, h, q, on_vector=False):
-            x0_t[G, h, q] = work.tile([P, SPAN, 2], BF16, name="x0_t", bufs=4)
-            copy = nc.vector.tensor_copy if on_vector else nc.scalar.copy
-            copy(out=x0_t[G, h, q][:].rearrange("p c e -> p (c e)").bitcast(F32), in_=x0_bank[G, h, q][:].rearrange("p i m -> p (i m)"))
+        def turn_x0(G, h, q, first_bank):
+            x0_bank[G, h, q] = take_bank(first_bank + q, [P, 2, SPAN], BF16)
+            for jj in range(2):
+                col = G * SPAN + (2 * q + jj) * P
+                for i in range(TILES):
+                    nc.tensor.transpose(x0_bank[G, h, q][:, jj, i * P : (i + 1) * P], x0_sb[h][:, i, col : col + P], ident16[:])
+
+        def empty_x0(G, h, q):
+            x0_t[G, h, q] = work.tile([P, 2, SPAN], BF16, name="x0_t", bufs=4)
+            nc.scalar.copy(out=x0_t[G, h, q][:], in_=x0_bank[G, h, q][:])
 
         def multiply(G, h, j, g, bank):
             done[G, h, j] = done.get((G, h, j), 0) + 1
@@ -160,11 +160,30 @@ def tile_centred_store_feature_cross_b15_kernel(tc, F_bytes, F_scale, F_mean, W,
             for g in range(PASSES):
                 multiply(G, h, j, g, bank)
 
+        def multiply_rows(G, h, i, g, bank):
+            done[G, h, i] = done.get((G, h, i), 0) + 1
+            if done[G, h, i] == 1:
+                acc[G, h, i] = take_bank(bank, [P, SPAN], F32)
+            rows = slice(i * P, (i + 1) * P)
+            nc.tensor.matmul_mx(
+                out=acc[G, h, i][:],
+                lhsT=codes["f", h, g][:, rows].bitcast(FP8X4), lhsT_scale=scales["f", h, g][:, rows],
+                rhs=codes["w", G, g][:].bitcast(FP8X4), rhs_scale=scales["w", G, g][:],
+                start=(done[G, h, i] == 1), stop=(done[G, h, i] == PASSES),
+            )
+
+        def add_b(G, h, i):
+            v_t[G, h, i] = work.tile([P, SPAN], F32, name="v_t", bufs=8)
+            nc.vector.tensor_tensor(out=v_t[G, h, i][:], in0=acc[G, h, i][:], in1=b_spread[:], op=ALU.add)
+
+        def times_x0(G, h, i):
+            nc.vector.tensor_tensor(out=v_t[G, h, i][:], in0=v_t[G, h, i][:], in1=x0_sb[h][:, i, G * SPAN : (G + 1) * SPAN], op=ALU.mult)
+
         def cross(G, h, j):
             v_t[G, h, j] = work.tile([P, SPAN], F32, name="v_t", bufs=8)
             nc.vector.scalar_tensor_tensor(
-                out=v_t[G, h, j][:], in0=acc[G, h, j][:], scalar=b_cols[:, 2 * G + j // 2, j % 2 : j % 2 + 1],
-                in1=x0_t[G, h, j // 2][:, :, j % 2], op0=ALU.add, op1=ALU.mult,
+                out=v_t[G, h, j][:], in0=acc[G, h, j][:], scalar=b_cols[:, G * TILES + j : G * TILES + j + 1],
+                in1=x0_t[G, h, j // 2][:, j % 2, :], op0=ALU.add, op1=ALU.mult,
             )
 
         def turn_back(G, h, i, bank):
@@ -172,19 +191,14 @@ def tile_centred_store_feature_cross_b15_kernel(tc, F_bytes, F_scale, F_mean, W,
             for j in range(TILES):
                 nc.tensor.transpose(y_bank[G, h, i][:, j * P : (j + 1) * P], v_t[G, h, j][:, i * P : (i + 1) * P], ident32[:])
 
-        def add_x(G, h, i):
+        def add_x(G, h, i, rows_form=False):
             y_sb[G, h, i] = work.tile([P, SPAN], F32, name="y_sb", bufs=YB)
-            nc.vector.tensor_tensor(
-                out=y_sb[G, h, i][:].rearrange("p (q m e) -> p q m e", q=2, e=2),
-                in0=y_bank[G, h, i][:].rearrange("p (q e m) -> p q m e", q=2, e=2),
-                in1=x_sb[h][:, i, G * SPAN : (G + 1) * SPAN].rearrange("p (q m e) -> p q m e", q=2, e=2),
-                op=ALU.add,
-            )
+            nc.vector.tensor_tensor(out=y_sb[G, h, i][:], in0=(v_t if rows_form else y_bank)[G, h, i][:], in1=x_sb[h][:, i, G * SPAN : (G + 1) * SPAN], op=ALU.add)
             row = h * SPAN + i * P
             nc.sync.dma_start(out=out_0[row : row + P, G * SPAN : (G + 1) * SPAN], in_=y_sb[G, h, i][:])
 
         def round_y(G, h, i, on_vector=False):
-            y16[G, h, i] = work.tile([P, 2, P, 2], BF16, name="y16", bufs=10)
+            y16[G, h, i] = work.tile([P, 2, P, 2], BF16, name="y16", bufs=8)
             copy = nc.vector.tensor_copy if on_vector else nc.scalar.copy
             copy(out=y16[G, h, i][:], in_=y_sb[G, h, i][:].rearrange("p (m u e) -> p u m e", u=2, e=2))
 
@@ -204,7 +218,7 @@ def tile_centred_store_feature_cross_b15_kernel(tc, F_bytes, F_scale, F_mean, W,
             copy(out=dst.rearrange("p (i m u) -> p i m u", i=count, u=2), in_=yt_bank[G, h, first][:].rearrange("p i u m -> p i m u"))
 
         def quantise_y(G, h, first, count):
-            y_codes = work.tile([P, count * P], U32, name="y_codes", bufs=5, align_bytes=64)
+            y_codes = work.tile([P, count * P], U32, name="y_codes", tag="y_codes%d" % count, bufs=3 if count == TILES else 2, align_bytes=64)
             rows = slice(h * SPAN + first * P, h * SPAN + (first + count) * P)
             nc.vector.quantize_mx(
                 out=y_codes[:].bitcast(FP8X4), scales=y_scales[:, G, rows],
@@ -212,6 +226,23 @@ def tile_centred_store_feature_cross_b15_kernel(tc, F_bytes, F_scale, F_mean, W,
             )
             dst = out_1[G, :, rows, :].rearrange("p m t -> p (m t)")
             nc.sync.dma_start(out=dst.bitcast(I32), in_=y_codes[:].bitcast(I32))
+
+        SF2 = True
+        def rows_pass(G, h, g, first, count, bank):
+            for i in range(first, first + count):
+                multiply_rows(G, h, i, g, bank + i - first)
+
+        def rows_tile(G, h, i, bank):
+            for g in range(PASSES):
+                multiply_rows(G, h, i, g, bank)
+
+        def rows2(G, h, first):
+            add_b(G, h, first)
+            add_b(G, h, first + 1)
+            times_x0(G, h, first)
+            times_x0(G, h, first + 1)
+            add_x(G, h, first, True)
+            add_x(G, h, first + 1, True)
 
         A, B, C = 0, 4, 6
 
@@ -247,15 +278,18 @@ def tile_centred_store_feature_cross_b15_kernel(tc, F_bytes, F_scale, F_mean, W,
             empty_y(G, h, 0, 2)
             empty_y(G, h, 2, 2)
 
-        nc.scalar.activation(out=b_cols[:], in_=b16[:], func=ACT.Identity)
+        nc.scalar.activation(out=ident16[:], in_=ident32[:], func=ACT.Identity)
         widen(0, 0)
         turn_f(0, 0, A)
         widen(0, 1)
         turn_f(0, 1, A + 2)
         affine(0, 0)
         widen(0, 2)
+        b_bank = take_bank(A, [P, P], BF16)
+        nc.tensor.transpose(b_bank[:], b_rows[:], ident16[:])
         turn_f(0, 2, B)
         affine(0, 1)
+        nc.scalar.copy(out=b_cols[:], in_=b_bank[:, 0 : N // P])
         widen(0, 3)
         turn_f(0, 3, C)
         interleave(("w", 0, 0))
@@ -279,7 +313,6 @@ def tile_centred_store_feature_cross_b15_kernel(tc, F_bytes, F_scale, F_mean, W,
         multiply_pass(0, 0, 1)
         turn_f(1, 0, C)
         empty_x0_both(0, 0)
-        turn_x0_both(1, 0, B)
         widen(1, 1)
         interleave(("f", 0, 2))
         quantise(("w", 1, 0))
@@ -288,100 +321,88 @@ def tile_centred_store_feature_cross_b15_kernel(tc, F_bytes, F_scale, F_mean, W,
         quantise(("f", 0, 3))
         multiply_pass(0, 0, 2)
         multiply_pass(0, 0, 3)
-        affine(1, 0)
-        empty_x0_both(1, 0)
         turn_f(1, 1, B)
+        affine(1, 0)
         interleave(("w", 1, 1))
+        interleave(("w", 1, 3), True)
         widen(1, 2)
         affine(1, 1)
         cross_all(0, 0)
-        multiply_pass(1, 0, 0)
+        rows_pass(1, 0, 0, 0, 4, A)
         quantise(("w", 1, 1))
         back2(0, 0, 0, C)
-        multiply_pass(1, 0, 1)
         interleave(("w", 1, 2))
-        interleave(("w", 1, 3))
+        quantise(("w", 1, 3))
+        rows_pass(1, 0, 1, 0, 4, A)
+        rows_pass(1, 0, 3, 0, 4, A)
+        add2(0, 0, 0)
         quantise(("w", 1, 2))
         turn_f(1, 2, B)
         widen(1, 3)
         affine(1, 2)
-        multiply_pass(1, 0, 2)
-        add2(0, 0, 0)
-        quantise(("w", 1, 3))
-        multiply_pass(1, 0, 3)
-        round2(0, 0, 0)
-        interleave(("f", 1, 0))
-        turn_f(1, 3, B)
+        rows_pass(1, 0, 2, 0, 4, A)
         back2(0, 0, 2, C)
-        affine(1, 3)
-        cross(1, 0, 0)
-        cross(1, 0, 1)
-        quantise(("f", 1, 0))
-        multiply(0, 1, 0, 0, A)
-        multiply(0, 1, 1, 0, A + 1)
+        interleave(("f", 1, 0))
         interleave(("f", 1, 1))
-        interleave(("f", 1, 3), True)
-        turn_x0_both(0, 1, B)
-        empty_x0_both(0, 1)
-        cross(1, 0, 2)
-        cross(1, 0, 3)
-        multiply(0, 1, 2, 0, A + 2)
-        multiply(0, 1, 3, 0, A + 3)
+        quantise(("f", 1, 0))
+        turn_f(1, 3, B)
+        affine(1, 3)
+        interleave(("f", 1, 2), SF2)
+        for i in range(TILES):
+            add_b(1, 0, i)
+        multiply_pass(0, 1, 0)
         quantise(("f", 1, 1))
-        multiply_pass(0, 1, 1)
+        interleave(("f", 1, 3), True)
         add2(0, 0, 2)
-        interleave(("f", 1, 2))
-        back2(1, 0, 0, C)
-        quantise(("f", 1, 3))
-        round2(0, 0, 2)
+        multiply_pass(0, 1, 1)
+        turn_x0_both(0, 1, C)
+        empty_x0_both(0, 1)
+        times_x0(1, 0, 0)
+        times_x0(1, 0, 1)
+        add_x(1, 0, 0, True)
+        add_x(1, 0, 1, True)
         quantise(("f", 1, 2))
         for g in (0, 1):
-            multiply(1, 1, 0, g, B)
-            multiply(1, 1, 1, g, B + 1)
-        add2(1, 0, 0)
-        multiply_pass(0, 1, 3)
+            rows_pass(1, 1, g, 0, 2, B)
         multiply_pass(0, 1, 2)
-        round2(1, 0, 0)
-        back2(1, 0, 2, C)
-        cross_all(0, 1)
-        turn_x0_both(1, 1, A)
-        empty_x0_both(1, 1)
-        for g in (3, 2):
-            multiply(1, 1, 0, g, B)
-            multiply(1, 1, 1, g, B + 1)
-        add2(1, 0, 2)
-        round2(1, 0, 2)
+        times_x0(1, 0, 2)
+        times_x0(1, 0, 3)
+        quantise(("f", 1, 3))
+        multiply_pass(0, 1, 3)
+        add_x(1, 0, 2, True)
+        add_x(1, 0, 3, True)
+        round2(0, 0, 0)
+        round2(0, 0, 2)
+        for g in (2, 3):
+            rows_pass(1, 1, g, 0, 2, B)
         turn_y_both(0, 0, C)
+        round2(1, 0, 0)
+        round2(1, 0, 2)
         empty_y_both(0, 0)
-        multiply_tile(1, 1, 2, A + 2)
-        cross(1, 1, 0)
-        cross(1, 1, 1)
+        cross_all(0, 1)
         back2(0, 1, 0, A)
-        multiply_tile(1, 1, 3, A + 3)
-        turn_y_both(1, 0, B)
+        rows_tile(1, 1, 2, A + 2)
+        rows2(1, 1, 0)
+        back2(0, 1, 2, B)
+        turn_y_both(1, 0, C)
+        rows_tile(1, 1, 3, A + 3)
+        round2(1, 1, 0)
         empty_y_both(1, 0)
-        back2(0, 1, 2, C)
-        quantise_y(0, 0, 0, 4)
         add2(0, 1, 0)
+        turn_y(1, 1, 0, 2, A)
         round2(0, 1, 0)
-        cross(1, 1, 2)
-        cross(1, 1, 3)
-        back2(1, 1, 0, A)
-        back2(1, 1, 2, A + 2)
         add2(0, 1, 2)
         round2(0, 1, 2)
-        turn_y_both(0, 1, B)
-        add2(1, 1, 0)
-        round2(1, 1, 0)
-        turn_y(1, 1, 0, 2, C)
-        empty_y_both(0, 1)
-        add2(1, 1, 2)
-        round2(1, 1, 2, True)
-        turn_y(1, 1, 2, 2, C + 1)
         empty_y(1, 1, 0, 2)
+        turn_y_both(0, 1, C)
+        empty_y_both(0, 1)
+        rows2(1, 1, 2)
+        round2(1, 1, 2, True)
+        turn_y(1, 1, 2, 2, A + 1)
+        quantise_y(0, 0, 0, 4)
         quantise_y(1, 0, 0, 4)
         quantise_y(0, 1, 0, 4)
-        empty_y(1, 1, 2, 2, True)
+        empty_y(1, 1, 2, 2)
         quantise_y(1, 1, 0, 2)
         quantise_y(1, 1, 2, 2)
         for q in range(4):

from contextlib import ExitStack

import concourse.mybir as mybir
from concourse.masks import make_identity

T, K, N = 1024, 2048, 1024
FLOPS = 2 * T * K * N

F32 = mybir.dt.float32
BF16 = mybir.dt.bfloat16
U32 = mybir.dt.uint32
I32 = mybir.dt.int32
U8 = mybir.dt.uint8
FP8 = mybir.dt.float8_e4m3fn
FP8X4 = mybir.dt.float8_e4m3fn_x4
ALU = mybir.AluOpType
ACT = mybir.ActivationFunctionType

P = 128
YB = 8
PB = 4
PACK = 4
SPAN = 512
PASSES = K // SPAN
TILES = SPAN // P


def tile_centred_store_feature_cross_b15_kernel(tc, F_bytes, F_scale, F_mean, W, b, x0, x, out_0, out_1, out_2):
    nc = tc.nc
    with ExitStack() as ctx:
        keep = ctx.enter_context(tc.tile_pool(name="keep", bufs=1))
        work = ctx.enter_context(tc.tile_pool(name="work", bufs=2))
        psum = ctx.enter_context(tc.psum_pool(name="psum", bufs=1))
        ctx.enter_context(tc.manual_schedule())

        def take_bank(number, shape, dtype):
            bank = psum.tile(shape, dtype, name="bank", tag="bank%d" % number)
            return bank

        ident32 = keep.tile([P, P], F32, name="ident32")
        ident16 = keep.tile([P, P], BF16, name="ident16")
        b_rows = keep.tile([P, P], BF16, name="b_rows")
        make_identity(nc, ident32[:])
        nc.gpsimd.memset(b_rows[:], 0.0)

        scale = keep.tile([P, PASSES, PACK], F32, name="scale")
        mean = keep.tile([P, PASSES, PACK], BF16, name="mean")
        b_cols = keep.tile([P, N // P], F32, name="b_cols")
        w_raw, f_raw, x0_sb, x_sb = {}, {}, {}, {}

        def load_w(G, g):
            w_raw[G, g] = keep.tile([P, PACK, SPAN], BF16, name="w_raw", bufs=2 * PASSES)
            src = W[g * SPAN : (g + 1) * SPAN, G * SPAN : (G + 1) * SPAN]
            nc.sync.dma_start(out=w_raw[G, g][:], in_=src.rearrange("(p t) n -> p t n", t=PACK))

        def load_f(h, g):
            f_raw[h, g] = keep.tile([P, TILES, SPAN], U8, name="f_raw", bufs=2 * PASSES)
            src = F_bytes[h * SPAN : (h + 1) * SPAN, g * SPAN : (g + 1) * SPAN]
            nc.sync.dma_start(out=f_raw[h, g][:], in_=src.rearrange("(i p) k -> p i k", p=P))

        def load_rows(store, src, name, h):
            store[h] = keep.tile([P, TILES, N], BF16, name=name, bufs=2)
            nc.sync.dma_start(out=store[h][:], in_=src[h * SPAN : (h + 1) * SPAN, :].rearrange("(i p) n -> p i n", p=P))

        load_w(0, 0)
        load_f(0, 0)
        load_f(0, 1)
        load_w(0, 1)
        nc.sync.dma_start(out=mean[:], in_=F_mean.rearrange("o (g p t) -> p (o g) t", p=P, t=PACK))
        nc.sync.dma_start(out=scale[:], in_=F_scale.rearrange("o (g p t) -> p (o g) t", p=P, t=PACK))
        nc.sync.dma_start(out=b_rows[0 : N // P, :], in_=b.rearrange("o (j p) -> (o j) p", p=P))
        for g in range(2, PASSES):
            load_w(0, g)
            load_f(0, g)
        load_rows(x0_sb, x0, "x0_sb", 0)
        for g in range(PASSES):
            load_w(1, g)
            load_f(1, g)
        load_rows(x_sb, x, "x_sb", 0)
        b_spread = keep.tile([P, SPAN], BF16, name="b_spread")
        nc.sync.dma_start(out=b_spread[:], in_=b[:, SPAN:N].rearrange("o n -> (o n)").partition_broadcast(P))
        load_rows(x0_sb, x0, "x0_sb", 1)
        load_rows(x_sb, x, "x_sb", 1)


        wide, f_banks, planes, grouped = {}, {}, {}, {}
        codes, scales = {}, {}
        x0_bank, yt_bank, done = {}, {}, {}
        x0_t, acc, v_t, y_bank, y_sb, y16, y_grouped = {}, {}, {}, {}, {}, {}, {}
        y_scales = keep.tile([P, N // SPAN, T], U8, name="y_scales", align_bytes=64)

        def widen(h, g, on_vector=False):
            wide[h, g] = work.tile([P, TILES, SPAN], BF16, name="wide", bufs=3)
            copy = nc.vector.tensor_copy if on_vector else nc.scalar.copy
            copy(out=wide[h, g][:], in_=f_raw[h, g][:].bitcast(FP8))

        def turn_f(h, g, first_bank):
            for u in range(2):
                f_banks[h, g, u] = take_bank(first_bank + u, [P, TILES, P], F32)
                for i in range(TILES):
                    words = wide[h, g][:, i, :].bitcast(F32)
                    nc.tensor.transpose(f_banks[h, g, u][:, i, :], words[:, u : 2 * P : 2], ident32[:])

        def affine(h, g):
            planes["f", h, g] = work.tile([P, PACK, SPAN], BF16, name="f_planes", bufs=PB)
            for u in range(2):
                pairs = f_banks[h, g, u][:].rearrange("p i m -> p (i m)").bitcast(BF16).rearrange("p (c e) -> p e c", e=2)
                for e in range(2):
                    t = 2 * u + e
                    nc.scalar.activation(
                        out=planes["f", h, g][:, t, :], in_=pairs[:, e, :], func=ACT.Identity,
                        scale=scale[:, g, t : t + 1], bias=mean[:, g, t : t + 1],
                    )

        def interleave(key, on_scalar=False):
            src = w_raw[key[1:]] if key[0] == "w" else planes[key]
            grouped[key] = work.tile([P, SPAN, PACK], BF16, name="grouped", bufs=3, align_bytes=64)
            if on_scalar:
                nc.scalar.copy(out=grouped[key][:], in_=src[:].rearrange("p t c -> p c t"))
            else:
                nc.vector.tensor_copy(
                    out=grouped[key][:].rearrange("p (c i) t -> p c t i", i=4),
                    in_=src[:].rearrange("p t (c i) -> p c t i", i=4),
                )

        def quantise(key):
            codes[key] = keep.tile([P, SPAN], U32, name="codes", bufs=4 * PASSES, align_bytes=64)
            scales[key] = keep.tile([P, SPAN], U8, name="scales", bufs=4 * PASSES, align_bytes=64)
            nc.vector.quantize_mx(out=codes[key][:].bitcast(FP8X4), scales=scales[key][:], in_=grouped[key][:].rearrange("p c t -> p (c t)"))


        def turn_x0(G, h, q, first_bank):
            x0_bank[G, h, q] = take_bank(first_bank + q, [P, 2, SPAN], BF16)
            for jj in range(2):
                col = G * SPAN + (2 * q + jj) * P
                for i in range(TILES):
                    nc.tensor.transpose(x0_bank[G, h, q][:, jj, i * P : (i + 1) * P], x0_sb[h][:, i, col : col + P], ident16[:])

        def empty_x0(G, h, q):
            x0_t[G, h, q] = work.tile([P, 2, SPAN], BF16, name="x0_t", bufs=4)
            nc.scalar.copy(out=x0_t[G, h, q][:], in_=x0_bank[G, h, q][:])

        def multiply(G, h, j, g, bank):
            done[G, h, j] = done.get((G, h, j), 0) + 1
            if done[G, h, j] == 1:
                acc[G, h, j] = take_bank(bank, [P, SPAN], F32)
            cols = slice(j * P, (j + 1) * P)
            nc.tensor.matmul_mx(
                out=acc[G, h, j][:],
                lhsT=codes["w", G, g][:, cols].bitcast(FP8X4), lhsT_scale=scales["w", G, g][:, cols],
                rhs=codes["f", h, g][:].bitcast(FP8X4), rhs_scale=scales["f", h, g][:],
                start=(done[G, h, j] == 1), stop=(done[G, h, j] == PASSES),
            )

        def multiply_pass(G, h, g):
            for j in range(TILES):
                multiply(G, h, j, g, j)

        def multiply_tile(G, h, j, bank):
            for g in range(PASSES):
                multiply(G, h, j, g, bank)

        def multiply_rows(G, h, i, g, bank):
            done[G, h, i] = done.get((G, h, i), 0) + 1
            if done[G, h, i] == 1:
                acc[G, h, i] = take_bank(bank, [P, SPAN], F32)
            rows = slice(i * P, (i + 1) * P)
            nc.tensor.matmul_mx(
                out=acc[G, h, i][:],
                lhsT=codes["f", h, g][:, rows].bitcast(FP8X4), lhsT_scale=scales["f", h, g][:, rows],
                rhs=codes["w", G, g][:].bitcast(FP8X4), rhs_scale=scales["w", G, g][:],
                start=(done[G, h, i] == 1), stop=(done[G, h, i] == PASSES),
            )

        def add_b(G, h, i):
            v_t[G, h, i] = work.tile([P, SPAN], F32, name="v_t", bufs=8)
            nc.vector.tensor_tensor(out=v_t[G, h, i][:], in0=acc[G, h, i][:], in1=b_spread[:], op=ALU.add)

        def times_x0(G, h, i):
            nc.vector.tensor_tensor(out=v_t[G, h, i][:], in0=v_t[G, h, i][:], in1=x0_sb[h][:, i, G * SPAN : (G + 1) * SPAN], op=ALU.mult)

        def cross(G, h, j):
            v_t[G, h, j] = work.tile([P, SPAN], F32, name="v_t", bufs=8)
            nc.vector.scalar_tensor_tensor(
                out=v_t[G, h, j][:], in0=acc[G, h, j][:], scalar=b_cols[:, G * TILES + j : G * TILES + j + 1],
                in1=x0_t[G, h, j // 2][:, j % 2, :], op0=ALU.add, op1=ALU.mult,
            )

        def turn_back(G, h, i, bank):
            y_bank[G, h, i] = take_bank(bank, [P, SPAN], F32)
            for j in range(TILES):
                nc.tensor.transpose(y_bank[G, h, i][:, j * P : (j + 1) * P], v_t[G, h, j][:, i * P : (i + 1) * P], ident32[:])

        def add_x(G, h, i, rows_form=False):
            y_sb[G, h, i] = work.tile([P, SPAN], F32, name="y_sb", bufs=YB)
            nc.vector.tensor_tensor(out=y_sb[G, h, i][:], in0=(v_t if rows_form else y_bank)[G, h, i][:], in1=x_sb[h][:, i, G * SPAN : (G + 1) * SPAN], op=ALU.add)
            row = h * SPAN + i * P
            nc.sync.dma_start(out=out_0[row : row + P, G * SPAN : (G + 1) * SPAN], in_=y_sb[G, h, i][:])

        def round_y(G, h, i, on_vector=False):
            y16[G, h, i] = work.tile([P, 2, P, 2], BF16, name="y16", bufs=8)
            copy = nc.vector.tensor_copy if on_vector else nc.scalar.copy
            copy(out=y16[G, h, i][:], in_=y_sb[G, h, i][:].rearrange("p (m u e) -> p u m e", u=2, e=2))

        def turn_y(G, h, first, count, number):
            bank = take_bank(number, [P, count, 2, P], F32)
            yt_bank[G, h, first] = bank
            for ii in range(count):
                for u in range(2):
                    words = y16[G, h, first + ii][:, u, :, :].rearrange("p m e -> p (m e)").bitcast(F32)
                    nc.tensor.transpose(bank[:, ii, u, :], words, ident32[:])

        def empty_y(G, h, first, count, on_vector=False):
            if first == 0:
                y_grouped[G, h] = work.tile([P, SPAN, PACK], BF16, name="y_grouped", bufs=4, align_bytes=64)
            dst = y_grouped[G, h][:, first * P : (first + count) * P, :].rearrange("p c t -> p (c t)").bitcast(F32)
            copy = nc.vector.tensor_copy if on_vector else nc.scalar.copy
            copy(out=dst.rearrange("p (i m u) -> p i m u", i=count, u=2), in_=yt_bank[G, h, first][:].rearrange("p i u m -> p i m u"))

        def quantise_y(G, h, first, count):
            y_codes = work.tile([P, count * P], U32, name="y_codes", tag="y_codes%d" % count, bufs=3 if count == TILES else 2, align_bytes=64)
            rows = slice(h * SPAN + first * P, h * SPAN + (first + count) * P)
            nc.vector.quantize_mx(
                out=y_codes[:].bitcast(FP8X4), scales=y_scales[:, G, rows],
                in_=y_grouped[G, h][:, first * P : (first + count) * P, :].rearrange("p c t -> p (c t)"),
            )
            dst = out_1[G, :, rows, :].rearrange("p m t -> p (m t)")
            nc.sync.dma_start(out=dst.bitcast(I32), in_=y_codes[:].bitcast(I32))

        SF2 = True
        def rows_pass(G, h, g, first, count, bank):
            for i in range(first, first + count):
                multiply_rows(G, h, i, g, bank + i - first)

        def rows_tile(G, h, i, bank):
            for g in range(PASSES):
                multiply_rows(G, h, i, g, bank)

        def rows2(G, h, first):
            add_b(G, h, first)
            add_b(G, h, first + 1)
            times_x0(G, h, first)
            times_x0(G, h, first + 1)
            add_x(G, h, first, True)
            add_x(G, h, first + 1, True)

        A, B, C = 0, 4, 6

        def cross_all(G, h):
            for j in range(TILES):
                cross(G, h, j)

        def back2(G, h, first, bank):
            turn_back(G, h, first, bank)
            turn_back(G, h, first + 1, bank + 1)

        def add2(G, h, first):
            add_x(G, h, first)
            add_x(G, h, first + 1)

        def round2(G, h, first, on_vector=False):
            round_y(G, h, first, on_vector)
            round_y(G, h, first + 1, on_vector)

        def turn_x0_both(G, h, bank):
            turn_x0(G, h, 0, bank)
            turn_x0(G, h, 1, bank)

        def empty_x0_both(G, h):
            empty_x0(G, h, 0)
            empty_x0(G, h, 1)

        def turn_y_both(G, h, bank):
            turn_y(G, h, 0, 2, bank)
            turn_y(G, h, 2, 2, bank + 1)

        def empty_y_both(G, h):
            empty_y(G, h, 0, 2)
            empty_y(G, h, 2, 2)

        nc.scalar.activation(out=ident16[:], in_=ident32[:], func=ACT.Identity)
        widen(0, 0)
        turn_f(0, 0, A)
        widen(0, 1)
        turn_f(0, 1, A + 2)
        affine(0, 0)
        widen(0, 2)
        b_bank = take_bank(A, [P, P], BF16)
        nc.tensor.transpose(b_bank[:], b_rows[:], ident16[:])
        turn_f(0, 2, B)
        affine(0, 1)
        nc.scalar.copy(out=b_cols[:], in_=b_bank[:, 0 : N // P])
        widen(0, 3)
        turn_f(0, 3, C)
        interleave(("w", 0, 0))
        quantise(("w", 0, 0))
        interleave(("w", 0, 1))
        interleave(("w", 0, 2))
        quantise(("w", 0, 1))
        interleave(("w", 0, 3))
        quantise(("w", 0, 2))
        interleave(("f", 0, 0))
        quantise(("w", 0, 3))
        affine(0, 2)
        interleave(("f", 0, 1))
        quantise(("f", 0, 0))
        multiply_pass(0, 0, 0)
        turn_x0_both(0, 0, B)
        affine(0, 3)
        widen(1, 0)
        interleave(("w", 1, 0))
        quantise(("f", 0, 1))
        multiply_pass(0, 0, 1)
        turn_f(1, 0, C)
        empty_x0_both(0, 0)
        widen(1, 1)
        interleave(("f", 0, 2))
        quantise(("w", 1, 0))
        interleave(("f", 0, 3))
        quantise(("f", 0, 2))
        quantise(("f", 0, 3))
        multiply_pass(0, 0, 2)
        multiply_pass(0, 0, 3)
        turn_f(1, 1, B)
        affine(1, 0)
        interleave(("w", 1, 1))
        interleave(("w", 1, 3), True)
        widen(1, 2)
        affine(1, 1)
        cross_all(0, 0)
        rows_pass(1, 0, 0, 0, 4, A)
        quantise(("w", 1, 1))
        back2(0, 0, 0, C)
        interleave(("w", 1, 2))
        quantise(("w", 1, 3))
        rows_pass(1, 0, 1, 0, 4, A)
        rows_pass(1, 0, 3, 0, 4, A)
        add2(0, 0, 0)
        quantise(("w", 1, 2))
        turn_f(1, 2, B)
        widen(1, 3)
        affine(1, 2)
        rows_pass(1, 0, 2, 0, 4, A)
        back2(0, 0, 2, C)
        interleave(("f", 1, 0))
        interleave(("f", 1, 1))
        quantise(("f", 1, 0))
        turn_f(1, 3, B)
        affine(1, 3)
        interleave(("f", 1, 2), SF2)
        for i in range(TILES):
            add_b(1, 0, i)
        multiply_pass(0, 1, 0)
        quantise(("f", 1, 1))
        interleave(("f", 1, 3), True)
        add2(0, 0, 2)
        multiply_pass(0, 1, 1)
        turn_x0_both(0, 1, C)
        empty_x0_both(0, 1)
        times_x0(1, 0, 0)
        times_x0(1, 0, 1)
        add_x(1, 0, 0, True)
        add_x(1, 0, 1, True)
        quantise(("f", 1, 2))
        for g in (0, 1):
            rows_pass(1, 1, g, 0, 2, B)
        multiply_pass(0, 1, 2)
        times_x0(1, 0, 2)
        times_x0(1, 0, 3)
        quantise(("f", 1, 3))
        multiply_pass(0, 1, 3)
        add_x(1, 0, 2, True)
        add_x(1, 0, 3, True)
        round2(0, 0, 0)
        round2(0, 0, 2)
        for g in (2, 3):
            rows_pass(1, 1, g, 0, 2, B)
        turn_y_both(0, 0, C)
        round2(1, 0, 0)
        round2(1, 0, 2)
        empty_y_both(0, 0)
        cross_all(0, 1)
        back2(0, 1, 0, A)
        rows_tile(1, 1, 2, A + 2)
        rows2(1, 1, 0)
        back2(0, 1, 2, B)
        turn_y_both(1, 0, C)
        rows_tile(1, 1, 3, A + 3)
        round2(1, 1, 0)
        empty_y_both(1, 0)
        add2(0, 1, 0)
        turn_y(1, 1, 0, 2, A)
        round2(0, 1, 0)
        add2(0, 1, 2)
        round2(0, 1, 2)
        empty_y(1, 1, 0, 2)
        turn_y_both(0, 1, C)
        empty_y_both(0, 1)
        rows2(1, 1, 2)
        round2(1, 1, 2, True)
        turn_y(1, 1, 2, 2, A + 1)
        quantise_y(0, 0, 0, 4)
        quantise_y(1, 0, 0, 4)
        quantise_y(0, 1, 0, 4)
        empty_y(1, 1, 2, 2)
        quantise_y(1, 1, 0, 2)
        quantise_y(1, 1, 2, 2)
        for q in range(4):
            dst = out_2[:, 4 * q : 4 * q + 4, :].rearrange("g r m -> r g m")
            nc.sync.dma_start(out=dst.bitcast(I32), in_=y_scales[32 * q : 32 * q + 4, :, :].bitcast(I32))
